import numpy as np
CORES = [2,6,18,22,34,38,50,54,66,70,82,86,98,102,114,118]
N = 16
ROOT = 9
def setup_inputs(rng):
    return {"x": rng.standard_normal((N, 128, 1024), dtype=np.float32)}
def reference(x):
    y = np.full(x.shape, np.nan, x.dtype)
    y[ROOT] = x.sum(axis=0, dtype=np.float64).astype(x.dtype)
    return {"y": y}

from concourse.bass import DstId, RemoteDMATransfer
from concourse.mybir import AluOpType

SCRATCH = {
    "x9": ("dram", [12, 128, 72], "float32"),
    "x10": ("dram", [2, 128, 80], "float32"),
    "m9": ("dram", [6, 128, 72], "float32"),
    "m10": ("dram", [128, 80], "float32"),
    "r9": ("dram", [6, 128, 72], "float32"),
    "r10": ("dram", [6, 128, 80], "float32"),
    "s9": ("dram", [12, 128, 72], "float32"),
    "s10": ("dram", [2, 128, 80], "float32"),
    "xf": ("dram", [128, 1024], "float32"),
    "pf": ("dram", [128, 1024], "float32"),
}
SEMAPHORES = ["loaded", "exch", "scat", "gath", "sent", "acc"]

N9 = 108
ALL16 = 0xFFFF
OFF8 = 0x00FF
CAP = 8192


def rank_program(g, core, T, topo):
    rank = T.rank_of(core)
    if rank is None:
        return
    root = T.cores[T.root]
    root_chip = topo.chip(root)
    chips = sorted(set(topo.chip(c) for c in T.cores))
    owners = [c for c in chips if c != root_chip]
    my_chip = topo.chip(core)
    h = 0 if core % 8 == 2 else 1
    mate = my_chip * 8 + (6 if h == 0 else 2)
    sem = T.sem

    def dst(c):
        rid, pid, _se = topo.addr(c)
        return DstId(rid=rid, pnc=pid)

    def piece(b9, b10, hh, k):
        return b9[hh * 6 + k] if k < 6 else b10[hh]

    def mate_piece(k):
        return T.m9[k] if k < 6 else T.m10[:]

    if core == root:
        g.dma_start(T.y[:, :], T.x[:, :]).then_inc(sem.acc, 16)
        g.wait_ge(sem.acc, 16)
        g.wait_ge(sem.exch, 16)
        g.dma_start(T.y[:, :], T.pf[:, :], accum_op=AluOpType.add, max_dma_last_dim=CAP).then_inc(sem.acc, 16)
        g.wait_ge(sem.acc, 32)
        g.wait_ge(sem.gath, 8 * 2 * len(owners))
        g.dma_start(T.y[0:N9, :], T.s9[:], accum_op=AluOpType.add, max_dma_last_dim=CAP).then_inc(sem.acc, 16)
        g.dma_start(T.y[N9:128, :], T.s10[:], accum_op=AluOpType.add, max_dma_last_dim=CAP).then_inc(sem.acc, 16)
        g.wait_ge(sem.acc, 64)
        return
    if my_chip == root_chip:
        g.sync.dma_start(T.xf[:, :], T.x[:, :]).then_inc(sem.loaded, 16)
        g.wait_ge(sem.loaded, 16)
        rid, pid, _se = topo.addr(root)
        g.remote_dma(T.pf[:, :], T.xf[:, :], sem.exch, sem.sent, pid, rid, ALL16)
        g.wait_ge(sem.sent, 16)
        return

    j = owners.index(my_chip)
    sent = 0
    g.sync.dma_start(T.x9[:], T.x[0:N9, :]).then_inc(sem.loaded, 16)
    g.scalar.dma_start(T.x10[:], T.x[N9:128, :]).then_inc(sem.loaded, 16)
    g.wait_ge(sem.loaded, 32)

    rid, pid, _se = topo.addr(mate)
    for k in range(7):
        out = T.m9[k] if k < 6 else T.m10[:]
        g.remote_dma(out, piece(T.x9, T.x10, 1 - h, k), sem.exch, sem.sent, pid, rid, ALL16)
        sent += 16
    g.wait_ge(sem.exch, 7 * 16)

    for d in range(1, 7):
        k = (j + d) % 7
        owner = owners[k] * 8 + core % 8
        slot = j if j < k else j - 1
        land = T.r9[slot] if k < 6 else T.r10[slot]
        g.remote_dma_fused(
            [RemoteDMATransfer(dst_ids=[dst(owner)], dma_engine_mask=OFF8, remote_sem=sem.scat,
                               srcs=[piece(T.x9, T.x10, h, k), mate_piece(k)], dsts=[land], alu_op=1)],
            local_sem=sem.sent)
        sent += 8
    g.wait_ge(sem.scat, 6 * 8)

    arrived = [(T.r9[s] if j < 6 else T.r10[s]) for s in range(6)]
    g.remote_dma_fused(
        [RemoteDMATransfer(dst_ids=[dst(root)], dma_engine_mask=OFF8, remote_sem=sem.gath,
                           srcs=[piece(T.x9, T.x10, h, j), mate_piece(j)] + arrived,
                           dsts=[piece(T.s9, T.s10, h, j)], alu_op=1)],
        local_sem=sem.sent)
    sent += 8
    g.wait_ge(sem.sent, sent)
